import numpy as np
import ml_dtypes


def mxq(x, axis, fmt="e4m3"):
    dtype, down = {"e4m3": (ml_dtypes.float8_e4m3fn, 7), "e5m2": (ml_dtypes.float8_e5m2, 14)}[fmt]
    v = np.moveaxis(np.asarray(x, np.float32).astype(ml_dtypes.bfloat16).astype(np.float64), axis, -1)
    blocks = v.reshape(v.shape[:-1] + (-1, 32))
    amax = np.abs(blocks).max(-1, keepdims=True)
    byte = np.maximum(np.where(amax > 0, np.frexp(amax)[1] - 1 + 127, 0) - down, 1)
    scale = np.exp2(byte - 127.0)
    codes = (blocks / scale).astype(np.float32).astype(dtype).astype(np.float64)
    return np.moveaxis((codes * scale).reshape(v.shape), -1, axis)


WIDE = False


def mx_kscale(k):
    if not WIDE:
        return np.ones(k)
    levels = np.array([10, -10, 5, -5, 0])
    if k % 512:
        return np.exp2(np.random.permutation(np.resize(levels, k // 32))).repeat(32)
    a = np.empty((k // 512, 16))
    for p in range(k // 512):
        a[p, :8] = np.random.permutation(np.resize(levels, 8))
        for g in range(8):
            far = levels[np.abs(levels - a[p, g]) >= 10]
            a[p, g + 8] = far[np.random.randint(len(far))]
    return np.exp2(a.ravel()).repeat(32)


def f64(x):
    return np.asarray(x).astype(np.float64)


def striped(idx):
    return np.tile(idx.reshape(-1, 16).T, (8, 1)).astype(np.uint16)


def unstriped(offs):
    return offs[:16].T.reshape(-1).astype(np.int64)


E2M1 = np.array([0.0, 0.5, 1.0, 1.5, 2.0, 3.0, 4.0, 6.0, -0.0, -0.5, -1.0, -1.5, -2.0, -3.0, -4.0, -6.0])


def pack_fp4(w):
    k, n = w.shape
    w = f64(np.asarray(w, np.float32).astype(ml_dtypes.bfloat16)).reshape(k // 32, 32, n)
    amax = np.abs(w).max(1)
    mant, ex = np.frexp(amax / 6.0)
    byte = np.clip(np.where(amax > 0, np.where(mant > 0.5, ex, ex - 1) + 127, 1), 1, 254)
    scaled = (w * np.exp2(127.0 - byte)[:, None, :]).reshape(k, n).astype(np.float32)
    c = np.ascontiguousarray(scaled.reshape(k // 512, 128, 4, n).transpose(0, 1, 3, 2)).astype(ml_dtypes.float4_e2m1fn).view(np.uint8) & 0xF
    words = (c[..., 0::2] | (c[..., 1::2] << 4)).reshape(k // 512, 128, 2 * n)
    return np.ascontiguousarray(words), np.ascontiguousarray(byte.astype(np.uint8).reshape(k // 512, 16, n))


def unpack_fp4(words, scales):
    g, _, n = scales.shape
    words = np.ascontiguousarray(words).reshape(g, 128, n, 2)
    nib = np.empty((g, 128, n, 4), np.uint8)
    nib[..., 0::2] = words & 0xF
    nib[..., 1::2] = words >> 4
    vals = E2M1[nib] * np.repeat(np.exp2(scales.astype(np.float64) - 127.0), 8, axis=1)[..., None]
    return vals.transpose(0, 1, 3, 2).reshape(g * 512, n)


def gelu(v):
    return 0.5 * v * (1.0 + np.tanh(np.sqrt(2.0 / np.pi) * (v + 0.044715 * v**3)))


K, T, S, V, H, N, J = 512, 2048, 1024, 512, 512, 256, 512


def setup_inputs():
    n = np.random.standard_normal
    s = mx_kscale(K)[:, None]
    u = mx_kscale(H)
    r = mx_kscale(J)[:, None]
    packed_w4 = pack_fp4(n((H, N)) / np.sqrt(H) / u[:, None])
    return {
        "xT": (n((K, T)) * s).astype(np.float32),
        "eT": (n((J, V)) * r).astype(np.float32),
        "w1": (n((K, H)) / np.sqrt(3 * K) / s * u).astype(np.float32),
        "w2": (n((K, H)) / np.sqrt(3 * K) / s * u).astype(np.float32),
        "w3": (n((J, H)) / np.sqrt(3 * J) / r * u).astype(np.float32),
        "w4_words": packed_w4[0],
        "w4_scales": packed_w4[1],
        "offs": striped(np.random.permutation(T)[:S]),
    }


def reference(xT, eT, w1, w2, w3, w4_words, w4_scales, offs):
    xq = mxq(f64(xT)[:, unstriped(offs)], 0, "e4m3")
    h = gelu(mxq(f64(w1), 0, "e4m3").T @ xq[:, :V] + mxq(f64(w2), 0, "e4m3").T @ xq[:, V:2 * V] + mxq(f64(w3), 0, "e4m3").T @ mxq(f64(eT), 0, "e4m3"))
    return unpack_fp4(w4_words, w4_scales).T @ mxq(h, 0, "e4m3")

@@ -1,0 +1,206 @@
+from contextlib import ExitStack
+
+import concourse.mybir as mybir
+
+K, T, V, H, N = 512, 2048, 512, 512, 256
+FLOPS = 2 * 3 * K * H * V + 2 * H * N * V
+
+F32 = mybir.dt.float32
+BF16 = mybir.dt.bfloat16
+I32 = mybir.dt.int32
+U32 = mybir.dt.uint32
+U16 = mybir.dt.uint16
+U8 = mybir.dt.uint8
+FP8X4 = mybir.dt.float8_e4m3fn_x4
+FP4X4 = mybir.dt.float4_e2m1fn_x4
+COPY = mybir.ActivationFunctionType.Copy
+GELU = mybir.ActivationFunctionType.Gelu_apprx_tanh
+
+P = 128
+PACK = 4
+EDGES = 128
+CHUNKS = V // EDGES
+X_PIECES = ((1024, 1024), (1024, 512, 512))
+
+
+def tile_picked_edgeup_gelu_e_kernel(tc, xT, eT, w1, w2, w3, w4_words, w4_scales, offs, out):
+    nc = tc.nc
+
+    def cast(on_vector, dst, src):
+        if on_vector:
+            nc.vector.tensor_copy(out=dst, in_=src)
+        else:
+            nc.scalar.activation(out=dst, in_=src, func=COPY)
+
+    with ExitStack() as ctx:
+        keep = ctx.enter_context(tc.tile_pool(name="keep", bufs=1))
+        psum = ctx.enter_context(tc.psum_pool(name="psum", bufs=1))
+
+        offsets = keep.tile([P, 2 * V // 16], U16, name="offsets")
+        nc.sync.dma_start(offsets[:], offs)
+
+        w4_plane = keep.tile([P, N], U8, name="w4_plane", align_bytes=64)
+        nc.gpsimd.memset(w4_plane[:], 0)
+        for q in range(4):
+            nc.gpsimd.dma_start(
+                out=w4_plane[32 * q : 32 * q + 4, :].bitcast(I32),
+                in_=w4_scales[0, 4 * q : 4 * q + 4, :].bitcast(I32),
+            )
+
+        x_rows = xT.rearrange("(p j) c -> p j c", j=PACK)
+        x_raw = []
+        for u in range(2):
+            c0 = 0
+            for i, width in enumerate(X_PIECES[u]):
+                raw = keep.tile([P, 2, width], F32, name=f"x_raw{u}_{i}")
+                nc.sync.dma_start(out=raw[:], in_=x_rows[:, 2 * u : 2 * u + 2, c0 : c0 + width])
+                x_raw.append((u, c0, width, raw))
+                c0 = c0 + width
+        w_raw = []
+        for i, w in enumerate((w1, w2, w3)):
+            raw = keep.tile([P, PACK, H], F32, name=f"w_raw{i}")
+            nc.sync.dma_start(out=raw[:], in_=w.rearrange("(p j) c -> p j c", j=PACK))
+            w_raw.append(raw)
+        e_rows = eT.rearrange("(p j) c -> p j c", j=PACK)
+        e_raw = []
+        w4_codes = keep.tile([P, 2 * N], U8, name="w4_codes", align_bytes=64)
+        for c in range(CHUNKS):
+            raw = keep.tile([P, PACK, EDGES], F32, name=f"e_raw{c}")
+            nc.sync.dma_start(out=raw[:], in_=e_rows[:, :, c * EDGES : (c + 1) * EDGES])
+            e_raw.append(raw)
+            if c == 0:
+                nc.sync.dma_start(out=w4_codes[:].bitcast(I32), in_=w4_words[0].bitcast(I32))
+
+        pairs = [keep.tile([P, 2 * T], BF16, name=f"pairs{u}", align_bytes=64) for u in range(2)]
+        picked = [keep.tile([P, PACK * V], BF16, name=f"picked{s}", align_bytes=64) for s in range(2)]
+        x_codes = [keep.tile([P, V], U32, name=f"x_codes{s}", align_bytes=64) for s in range(2)]
+        x_scales = [keep.tile([P, V], U8, name=f"x_scales{s}", align_bytes=64) for s in range(2)]
+
+        def cast_piece(piece, vector_cols):
+            u, c0, width, raw = x_raw[piece]
+            dst = pairs[u][:].rearrange("p (c u) -> p c u", u=2)
+            src = raw[:].rearrange("p u c -> p c u")
+            cut = width - vector_cols
+            if cut > 0:
+                cast(False, dst[:, c0 : c0 + cut, :], src[:, 0:cut, :])
+            if vector_cols > 0:
+                cast(True, dst[:, c0 + cut : c0 + width, :], src[:, cut:width, :])
+
+        def gather(u, s):
+            words = picked[s][:].bitcast(U32).rearrange("p (v u) -> p v u", u=2)
+            nc.vector.tensor_copy(
+                out=words[:, :, u],
+                in_=pairs[u][:].bitcast(U32).indirect(offsets[:, s * (V // 16) : (s + 1) * (V // 16)]),
+            )
+
+        def quantize(codes, scales, values):
+            nc.vector.quantize_mx(out=codes.bitcast(FP8X4), scales=scales, in_=values)
+
+        cast_piece(0, 640)
+        cast_piece(1, 640)
+        gather(0, 0)
+        cast_piece(2, 0)
+        gather(0, 1)
+        cast_piece(3, 256)
+        cast_piece(4, 320)
+        gather(1, 0)
+        gather(1, 1)
+        for s in range(2):
+            quantize(x_codes[s][:], x_scales[s][:], picked[s][:])
+
+        w_grouped = [keep.tile([P, PACK * H], BF16, name=f"w_grouped{i}", align_bytes=64) for i in range(3)]
+        w_codes = [keep.tile([P, H], U32, name=f"w_codes{i}", align_bytes=64) for i in range(3)]
+        w_scales = [keep.tile([P, H], U8, name=f"w_scales{i}", align_bytes=64) for i in range(3)]
+
+        def deal(i, vector_m):
+            dst = w_grouped[i][:].rearrange("p (t m j) -> p m j t", t=PACK, j=PACK)
+            src = w_raw[i][:].rearrange("p j (m t) -> p m j t", t=PACK)
+            cut = P - vector_m
+            cast(False, dst[:, 0:cut], src[:, 0:cut])
+            if vector_m > 0:
+                cast(True, dst[:, cut:P], src[:, cut:P])
+
+        e_grouped = [keep.tile([P, PACK * EDGES], BF16, name=f"e_grouped{c}", align_bytes=64) for c in range(CHUNKS)]
+        e_codes = [keep.tile([P, EDGES], U32, name=f"e_codes{c}", align_bytes=64) for c in range(CHUNKS)]
+        e_scales = [keep.tile([P, EDGES], U8, name=f"e_scales{c}", align_bytes=64) for c in range(CHUNKS)]
+
+        def group_edges(c, on_vector):
+            dst = e_grouped[c][:].rearrange("p (c i j) -> p c j i", i=4, j=PACK)
+            src = e_raw[c][:].rearrange("p j (c i) -> p c j i", i=4)
+            cast(on_vector, dst, src)
+
+        hidden = [psum.tile([P, PACK * EDGES], F32, name=f"hidden{c}") for c in range(CHUNKS)]
+
+        def first_layer(c, t, term):
+            cols = slice(c * EDGES, (c + 1) * EDGES)
+            rows = slice(t * P, (t + 1) * P)
+            codes, scales = (x_codes[term][:, cols], x_scales[term][:, cols]) if term < 2 else (e_codes[c][:], e_scales[c][:])
+            nc.tensor.matmul_mx(
+                out=hidden[c][:, t * EDGES : (t + 1) * EDGES],
+                lhsT=w_codes[term][:, rows].bitcast(FP8X4),
+                lhsT_scale=w_scales[term][:, rows],
+                rhs=codes.bitcast(FP8X4),
+                rhs_scale=scales,
+                start=(term == 0),
+                stop=(term == 2),
+            )
+
+        deal(0, 0)
+        quantize(w_codes[0][:], w_scales[0][:], w_grouped[0][:])
+        for c in range(CHUNKS):
+            first_layer(c, 0, 0)
+        deal(1, 64)
+        quantize(w_codes[1][:], w_scales[1][:], w_grouped[1][:])
+        for c in range(CHUNKS):
+            first_layer(c, 0, 1)
+        deal(2, 80)
+        group_edges(0, False)
+        for t in range(PACK):
+            quantize(w_codes[2][:, t * P : (t + 1) * P], w_scales[2][:, t * P : (t + 1) * P], w_grouped[2][:, t * 512 : (t + 1) * 512])
+            if t == 0:
+                quantize(e_codes[0][:], e_scales[0][:], e_grouped[0][:])
+
+        h_grouped = [keep.tile([P, PACK * EDGES], BF16, name=f"h_grouped{c}", align_bytes=64) for c in range(CHUNKS)]
+        h_codes = [keep.tile([P, EDGES], U32, name=f"h_codes{c}", align_bytes=64) for c in range(CHUNKS)]
+        h_scales = [keep.tile([P, EDGES], U8, name=f"h_scales{c}", align_bytes=64) for c in range(CHUNKS)]
+        result = [psum.tile([P, 2 * EDGES], F32, name=f"result{c}") for c in range(CHUNKS)]
+        staged = [keep.tile([P, 2 * EDGES], F32, name=f"staged{c}") for c in range(CHUNKS)]
+        out_rows = out.rearrange("(m p) v -> p m v", p=P)
+
+        def finish_first(c):
+            first_layer(c, 0, 2)
+            for t in range(1, PACK):
+                for term in range(3):
+                    first_layer(c, t, term)
+            nc.scalar.activation(
+                out=h_grouped[c][:].rearrange("p (v t) -> p v t", t=PACK),
+                in_=hidden[c][:].rearrange("p (t v) -> p v t", t=PACK),
+                func=GELU,
+            )
+
+        def second_layer(c):
+            quantize(h_codes[c][:], h_scales[c][:], h_grouped[c][:])
+            for m in range(2):
+                nc.tensor.matmul_mx(
+                    out=result[c][:, m * EDGES : (m + 1) * EDGES],
+                    lhsT=w4_codes[:, 2 * m * P : 2 * (m + 1) * P].bitcast(FP4X4),
+                    lhsT_scale=w4_plane[:, m * P : (m + 1) * P],
+                    rhs=h_codes[c][:].bitcast(FP8X4),
+                    rhs_scale=h_scales[c][:],
+                    start=True,
+                    stop=True,
+                )
+            nc.vector.tensor_copy(out=staged[c][:], in_=result[c][:])
+            nc.sync.dma_start(
+                out=out_rows[:, :, c * EDGES : (c + 1) * EDGES],
+                in_=staged[c][:].rearrange("p (m v) -> p m v", m=2),
+            )
+
+        for c in range(CHUNKS):
+            if c + 1 < CHUNKS:
+                group_edges(c + 1, c >= 1)
+                quantize(e_codes[c + 1][:], e_scales[c + 1][:], e_grouped[c + 1][:])
+            finish_first(c)
+            if c >= 1:
+                second_layer(c - 1)
+        second_layer(CHUNKS - 1)

@@ -18,189 +18,204 @@ GELU = mybir.ActivationFunctionType.Gelu_apprx_tanh
 
 P = 128
 PACK = 4
+LINE = 4
 EDGES = 128
 CHUNKS = V // EDGES
-X_PIECES = ((1024, 1024), (1024, 512, 512))
+SRC, DST, EDGE = 0, 1, 2
+
+X_LAST = 512
+X_WIDTHS = ((T - X_LAST) // 2, (T - X_LAST) // 2, X_LAST)
+E_WIDTHS = (2 * EDGES, EDGES, EDGES)
+
+FREE_SHARE = 11
+X_MIDDLE_ON_VECTOR = 256
+W_ON_VECTOR = (0, 48, 64)
 
 
 def tile_picked_edgeup_gelu_e_kernel(tc, xT, eT, w1, w2, w3, w4_words, w4_scales, offs, out):
     nc = tc.nc
 
-    def cast(on_vector, dst, src):
+    def copy(on_vector, dst, src):
         if on_vector:
             nc.vector.tensor_copy(out=dst, in_=src)
         else:
             nc.scalar.activation(out=dst, in_=src, func=COPY)
+
+    def shared_copy(dst, src, on_vector):
+        count = src.shape[1]
+        cut = count - on_vector
+        copy(False, dst[:, 0:cut], src[:, 0:cut])
+        if on_vector > 0:
+            copy(True, dst[:, cut:count], src[:, cut:count])
+
+    def quantize(codes, scales, values):
+        nc.vector.quantize_mx(out=codes.bitcast(FP8X4), scales=scales, in_=values)
+
+    def weave(dst, first_and_second):
+        nc.vector.tensor_copy(out=dst.bitcast(I32).rearrange("p (n u) -> p n u", u=2), in_=first_and_second)
 
     with ExitStack() as ctx:
         keep = ctx.enter_context(tc.tile_pool(name="keep", bufs=1))
         psum = ctx.enter_context(tc.psum_pool(name="psum", bufs=1))
 
         offsets = keep.tile([P, 2 * V // 16], U16, name="offsets")
-        nc.sync.dma_start(offsets[:], offs)
 
-        w4_plane = keep.tile([P, N], U8, name="w4_plane", align_bytes=64)
-        nc.gpsimd.memset(w4_plane[:], 0)
-        for q in range(4):
-            nc.gpsimd.dma_start(
-                out=w4_plane[32 * q : 32 * q + 4, :].bitcast(I32),
+        warm = keep.tile([P, 2], F32, name="warm")
+        nc.vector.memset(warm[:, 0:1], 0.0)
+        nc.scalar.activation(out=warm[:, 1:2], in_=warm[:, 0:1], func=GELU)
+
+        planes = keep.tile([P, H], U8, name="planes", align_bytes=64)
+        for q in range(P // 32):
+            nc.scalar.dma_start(
+                out=planes[32 * q : 32 * q + 4, 0:N].bitcast(I32),
                 in_=w4_scales[0, 4 * q : 4 * q + 4, :].bitcast(I32),
             )
 
         x_rows = xT.rearrange("(p j) c -> p j c", j=PACK)
-        x_raw = []
-        for u in range(2):
-            c0 = 0
-            for i, width in enumerate(X_PIECES[u]):
-                raw = keep.tile([P, 2, width], F32, name=f"x_raw{u}_{i}")
-                nc.sync.dma_start(out=raw[:], in_=x_rows[:, 2 * u : 2 * u + 2, c0 : c0 + width])
-                x_raw.append((u, c0, width, raw))
-                c0 = c0 + width
-        w_raw = []
-        for i, w in enumerate((w1, w2, w3)):
-            raw = keep.tile([P, PACK, H], F32, name=f"w_raw{i}")
-            nc.sync.dma_start(out=raw[:], in_=w.rearrange("(p j) c -> p j c", j=PACK))
-            w_raw.append(raw)
-        e_rows = eT.rearrange("(p j) c -> p j c", j=PACK)
-        e_raw = []
+        x_low = keep.tile([P, 2, T], F32, name="x_low")
+        nc.sync.dma_start(out=x_low[:], in_=x_rows[:, 0:2, :])
+        nc.sync.dma_start(offsets[:], offs)
+        x_ranges = [slice(sum(X_WIDTHS[:r]), sum(X_WIDTHS[: r + 1])) for r in range(len(X_WIDTHS))]
+        x_high = []
+        for r, width in enumerate(X_WIDTHS):
+            x_high.append(keep.tile([P, 2, width], F32, name=f"x_high{r}"))
+            nc.sync.dma_start(out=x_high[r][:], in_=x_rows[:, 2:4, x_ranges[r]])
+
+        w_raw = [keep.tile([P, PACK, H], F32, name=f"w_raw{n}") for n in (SRC, DST, EDGE)]
+        e_raw = [keep.tile([P, PACK, width], F32, name=f"e_raw{r}") for r, width in enumerate(E_WIDTHS)]
         w4_codes = keep.tile([P, 2 * N], U8, name="w4_codes", align_bytes=64)
-        for c in range(CHUNKS):
-            raw = keep.tile([P, PACK, EDGES], F32, name=f"e_raw{c}")
-            nc.sync.dma_start(out=raw[:], in_=e_rows[:, :, c * EDGES : (c + 1) * EDGES])
-            e_raw.append(raw)
-            if c == 0:
-                nc.sync.dma_start(out=w4_codes[:].bitcast(I32), in_=w4_words[0].bitcast(I32))
+        for n, w in enumerate((w1, w2, w3)):
+            nc.sync.dma_start(out=w_raw[n][:], in_=w.rearrange("(p j) c -> p j c", j=PACK))
+        e_rows = eT.rearrange("(p j) c -> p j c", j=PACK)
+        for r, width in enumerate(E_WIDTHS):
+            first = sum(E_WIDTHS[:r])
+            nc.sync.dma_start(out=e_raw[r][:], in_=e_rows[:, :, first : first + width])
+        nc.sync.dma_start(out=w4_codes[:].bitcast(I32), in_=w4_words[0].bitcast(I32))
 
         pairs = [keep.tile([P, 2 * T], BF16, name=f"pairs{u}", align_bytes=64) for u in range(2)]
-        picked = [keep.tile([P, PACK * V], BF16, name=f"picked{s}", align_bytes=64) for s in range(2)]
-        x_codes = [keep.tile([P, V], U32, name=f"x_codes{s}", align_bytes=64) for s in range(2)]
-        x_scales = [keep.tile([P, V], U8, name=f"x_scales{s}", align_bytes=64) for s in range(2)]
+        picked = [keep.tile([P, PACK * V], BF16, name=f"picked{n}", align_bytes=64) for n in (SRC, DST)]
+        x_codes = [keep.tile([P, V], U32, name=f"x_codes{n}", align_bytes=64) for n in (SRC, DST)]
+        x_scales = [keep.tile([P, V], U8, name=f"x_scales{n}", align_bytes=64) for n in (SRC, DST)]
+        gathered = keep.tile([P, 2 * 2 * V], U32, name="gathered")
 
-        def cast_piece(piece, vector_cols):
-            u, c0, width, raw = x_raw[piece]
-            dst = pairs[u][:].rearrange("p (c u) -> p c u", u=2)
-            src = raw[:].rearrange("p u c -> p c u")
-            cut = width - vector_cols
-            if cut > 0:
-                cast(False, dst[:, c0 : c0 + cut, :], src[:, 0:cut, :])
-            if vector_cols > 0:
-                cast(True, dst[:, c0 + cut : c0 + width, :], src[:, cut:width, :])
+        def round_pairs(u, nodes, raw, on_vector):
+            dst = pairs[u][:].rearrange("p (c a) -> p c a", a=2)[:, nodes, :]
+            shared_copy(dst, raw[:].rearrange("p a c -> p c a"), on_vector)
 
-        def gather(u, s):
-            words = picked[s][:].bitcast(U32).rearrange("p (v u) -> p v u", u=2)
+        def gather(u, begin, end):
             nc.vector.tensor_copy(
-                out=words[:, :, u],
-                in_=pairs[u][:].bitcast(U32).indirect(offsets[:, s * (V // 16) : (s + 1) * (V // 16)]),
+                out=gathered[:, u * 2 * V + begin : u * 2 * V + end],
+                in_=pairs[u][:].bitcast(U32).indirect(offsets[:, begin // 16 : end // 16]),
             )
 
-        def quantize(codes, scales, values):
-            nc.vector.quantize_mx(out=codes.bitcast(FP8X4), scales=scales, in_=values)
+        round_pairs(0, slice(0, T), x_low, T * FREE_SHARE // 16)
+        gather(0, 0, 2 * V)
+        for r, on_vector in enumerate((0, X_MIDDLE_ON_VECTOR, X_LAST * FREE_SHARE // 16)):
+            round_pairs(1, x_ranges[r], x_high[r], on_vector)
+        for n in (SRC, DST):
+            gather(1, n * V, (n + 1) * V)
+        both_pairs = gathered[:].bitcast(I32).rearrange("p (u n) -> p n u", u=2)
+        for n in (SRC, DST):
+            weave(picked[n][:], both_pairs[:, n * V : (n + 1) * V, :])
+        for n in (SRC, DST):
+            quantize(x_codes[n][:], x_scales[n][:], picked[n][:])
 
-        cast_piece(0, 640)
-        cast_piece(1, 640)
-        gather(0, 0)
-        cast_piece(2, 0)
-        gather(0, 1)
-        cast_piece(3, 256)
-        cast_piece(4, 320)
-        gather(1, 0)
-        gather(1, 1)
-        for s in range(2):
-            quantize(x_codes[s][:], x_scales[s][:], picked[s][:])
-
-        w_grouped = [keep.tile([P, PACK * H], BF16, name=f"w_grouped{i}", align_bytes=64) for i in range(3)]
-        w_codes = [keep.tile([P, H], U32, name=f"w_codes{i}", align_bytes=64) for i in range(3)]
-        w_scales = [keep.tile([P, H], U8, name=f"w_scales{i}", align_bytes=64) for i in range(3)]
-
-        def deal(i, vector_m):
-            dst = w_grouped[i][:].rearrange("p (t m j) -> p m j t", t=PACK, j=PACK)
-            src = w_raw[i][:].rearrange("p j (m t) -> p m j t", t=PACK)
-            cut = P - vector_m
-            cast(False, dst[:, 0:cut], src[:, 0:cut])
-            if vector_m > 0:
-                cast(True, dst[:, cut:P], src[:, cut:P])
-
+        w_grouped = [keep.tile([P, PACK * H], BF16, name=f"w_grouped{n}", align_bytes=64) for n in (SRC, DST, EDGE)]
+        w_codes = [keep.tile([P, H], U32, name=f"w_codes{n}", align_bytes=64) for n in (SRC, DST, EDGE)]
+        w_scales = [planes[4:P, :]] + [keep.tile([P, H], U8, name=f"w_scales{n}", align_bytes=64)[:] for n in (DST, EDGE)]
         e_grouped = [keep.tile([P, PACK * EDGES], BF16, name=f"e_grouped{c}", align_bytes=64) for c in range(CHUNKS)]
         e_codes = [keep.tile([P, EDGES], U32, name=f"e_codes{c}", align_bytes=64) for c in range(CHUNKS)]
         e_scales = [keep.tile([P, EDGES], U8, name=f"e_scales{c}", align_bytes=64) for c in range(CHUNKS)]
+        e_chunks = [e_raw[r][:, :, first : first + EDGES] for r, width in enumerate(E_WIDTHS) for first in range(0, width, EDGES)]
 
-        def group_edges(c, on_vector):
-            dst = e_grouped[c][:].rearrange("p (c i j) -> p c j i", i=4, j=PACK)
-            src = e_raw[c][:].rearrange("p j (c i) -> p c j i", i=4)
-            cast(on_vector, dst, src)
+        def round_weights(n):
+            dst = w_grouped[n][:].rearrange("p (t m j) -> p m j t", t=PACK, j=PACK)
+            src = w_raw[n][:].rearrange("p j (m t) -> p m j t", t=PACK)
+            shared_copy(dst, src, W_ON_VECTOR[n])
 
-        hidden = [psum.tile([P, PACK * EDGES], F32, name=f"hidden{c}") for c in range(CHUNKS)]
+        def quantize_weights(n, t_begin, t_end):
+            cols = slice(t_begin * P, t_end * P)
+            quantize(w_codes[n][:, cols], w_scales[n][:, cols], w_grouped[n][:, PACK * t_begin * P : PACK * t_end * P])
 
-        def first_layer(c, t, term):
-            cols = slice(c * EDGES, (c + 1) * EDGES)
-            rows = slice(t * P, (t + 1) * P)
-            codes, scales = (x_codes[term][:, cols], x_scales[term][:, cols]) if term < 2 else (e_codes[c][:], e_scales[c][:])
+        def round_edges(c):
+            dst = e_grouped[c][:].rearrange("p (g a j) -> p g j a", a=LINE, j=PACK)
+            src = e_chunks[c].rearrange("p j (g a) -> p g j a", a=LINE)
+            copy(c in (0, CHUNKS - 1), dst, src)
+
+        def quantize_edges(c):
+            quantize(e_codes[c][:], e_scales[c][:], e_grouped[c][:])
+
+        banks = [f"bank{c}_{b}" for c in range(CHUNKS) for b in range(2)]
+        hidden = [[psum.tile([P, 2 * EDGES], F32, name=f"hidden{c}_{b}", tag=banks[2 * c + b]) for b in range(2)] for c in range(CHUNKS)]
+
+        def first_layer_pass(c, t, n):
+            edges = slice(c * EDGES, (c + 1) * EDGES)
+            cols = slice(t * P, (t + 1) * P)
+            codes, scales = (e_codes[c][:], e_scales[c][:]) if n == EDGE else (x_codes[n][:, edges], x_scales[n][:, edges])
             nc.tensor.matmul_mx(
-                out=hidden[c][:, t * EDGES : (t + 1) * EDGES],
-                lhsT=w_codes[term][:, rows].bitcast(FP8X4),
-                lhsT_scale=w_scales[term][:, rows],
+                out=hidden[c][t // 2][:, (t % 2) * EDGES : (t % 2 + 1) * EDGES],
+                lhsT=w_codes[n][:, cols].bitcast(FP8X4),
+                lhsT_scale=w_scales[n][:, cols],
                 rhs=codes.bitcast(FP8X4),
                 rhs_scale=scales,
-                start=(term == 0),
-                stop=(term == 2),
+                start=(n == SRC),
+                stop=(n == EDGE),
             )
 
-        deal(0, 0)
-        quantize(w_codes[0][:], w_scales[0][:], w_grouped[0][:])
-        for c in range(CHUNKS):
-            first_layer(c, 0, 0)
-        deal(1, 64)
-        quantize(w_codes[1][:], w_scales[1][:], w_grouped[1][:])
-        for c in range(CHUNKS):
-            first_layer(c, 0, 1)
-        deal(2, 80)
-        group_edges(0, False)
-        for t in range(PACK):
-            quantize(w_codes[2][:, t * P : (t + 1) * P], w_scales[2][:, t * P : (t + 1) * P], w_grouped[2][:, t * 512 : (t + 1) * 512])
-            if t == 0:
-                quantize(e_codes[0][:], e_scales[0][:], e_grouped[0][:])
+        for n in (SRC, DST):
+            round_weights(n)
+            quantize_weights(n, 0, PACK)
+            for c in range(CHUNKS):
+                for b in range(2):
+                    first_layer_pass(c, 2 * b, n)
+
+        round_weights(EDGE)
+        round_edges(0)
+        quantize_weights(EDGE, 0, 2)
+        quantize_edges(0)
+        quantize_weights(EDGE, 2, PACK)
+        for c in range(1, CHUNKS):
+            round_edges(c)
+            quantize_edges(c)
 
         h_grouped = [keep.tile([P, PACK * EDGES], BF16, name=f"h_grouped{c}", align_bytes=64) for c in range(CHUNKS)]
-        h_codes = [keep.tile([P, EDGES], U32, name=f"h_codes{c}", align_bytes=64) for c in range(CHUNKS)]
-        h_scales = [keep.tile([P, EDGES], U8, name=f"h_scales{c}", align_bytes=64) for c in range(CHUNKS)]
-        result = [psum.tile([P, 2 * EDGES], F32, name=f"result{c}") for c in range(CHUNKS)]
-        staged = [keep.tile([P, 2 * EDGES], F32, name=f"staged{c}") for c in range(CHUNKS)]
+        for c in range(CHUNKS):
+            h_pairs = keep.tile([P, PACK * EDGES], BF16, name=f"h_pairs{c}")
+            for b in range(2):
+                first_layer_pass(c, 2 * b, EDGE)
+                for n in (SRC, DST, EDGE):
+                    first_layer_pass(c, 2 * b + 1, n)
+                nc.scalar.activation(
+                    out=h_pairs[:, b * 2 * EDGES : (b + 1) * 2 * EDGES].rearrange("p (v a) -> p v a", a=2),
+                    in_=hidden[c][b][:].rearrange("p (a v) -> p v a", a=2),
+                    func=GELU,
+                )
+            weave(h_grouped[c][:], h_pairs[:].bitcast(I32).rearrange("p (b v) -> p v b", b=2))
+
         out_rows = out.rearrange("(m p) v -> p m v", p=P)
-
-        def finish_first(c):
-            first_layer(c, 0, 2)
-            for t in range(1, PACK):
-                for term in range(3):
-                    first_layer(c, t, term)
-            nc.scalar.activation(
-                out=h_grouped[c][:].rearrange("p (v t) -> p v t", t=PACK),
-                in_=hidden[c][:].rearrange("p (t v) -> p v t", t=PACK),
-                func=GELU,
-            )
-
-        def second_layer(c):
-            quantize(h_codes[c][:], h_scales[c][:], h_grouped[c][:])
-            for m in range(2):
+        for c in range(CHUNKS):
+            h_codes = keep.tile([P, EDGES], U32, name=f"h_codes{c}", align_bytes=64)
+            h_scales = keep.tile([P, EDGES], U8, name=f"h_scales{c}", align_bytes=64)
+            staged = keep.tile([P, 2 * EDGES], F32, name=f"staged{c}")
+            quantize(h_codes[:], h_scales[:], h_grouped[c][:])
+            last = c == CHUNKS - 1
+            results = [psum.tile([P, 2 * EDGES], F32, name=f"result{c}_{m}", tag=banks[c + m]) for m in range(2 if last else 1)]
+            for m in range(N // P):
+                cols = slice(m * EDGES, (m + 1) * EDGES)
                 nc.tensor.matmul_mx(
-                    out=result[c][:, m * EDGES : (m + 1) * EDGES],
+                    out=results[m if last else 0][:, cols],
                     lhsT=w4_codes[:, 2 * m * P : 2 * (m + 1) * P].bitcast(FP4X4),
-                    lhsT_scale=w4_plane[:, m * P : (m + 1) * P],
-                    rhs=h_codes[c][:].bitcast(FP8X4),
-                    rhs_scale=h_scales[c][:],
+                    lhsT_scale=planes[:, m * P : (m + 1) * P],
+                    rhs=h_codes[:].bitcast(FP8X4),
+                    rhs_scale=h_scales[:],
                     start=True,
                     stop=True,
                 )
-            nc.vector.tensor_copy(out=staged[c][:], in_=result[c][:])
+                if last:
+                    copy(m == 1, staged[:, cols], results[m][:, cols])
+            if not last:
+                copy(False, staged[:], results[0][:])
             nc.sync.dma_start(
                 out=out_rows[:, :, c * EDGES : (c + 1) * EDGES],
-                in_=staged[c][:].rearrange("p (m v) -> p m v", m=2),
+                in_=staged[:].rearrange("p (m v) -> p m v", m=2),
             )
-
-        for c in range(CHUNKS):
-            if c + 1 < CHUNKS:
-                group_edges(c + 1, c >= 1)
-                quantize(e_codes[c + 1][:], e_scales[c + 1][:], e_grouped[c + 1][:])
-            finish_first(c)
-            if c >= 1:
-                second_layer(c - 1)
-        second_layer(CHUNKS - 1)

from contextlib import ExitStack

import concourse.mybir as mybir

K, T, V, H, N = 512, 2048, 512, 512, 256
FLOPS = 2 * 3 * K * H * V + 2 * H * N * V

F32 = mybir.dt.float32
BF16 = mybir.dt.bfloat16
I32 = mybir.dt.int32
U32 = mybir.dt.uint32
U16 = mybir.dt.uint16
U8 = mybir.dt.uint8
FP8X4 = mybir.dt.float8_e4m3fn_x4
FP4X4 = mybir.dt.float4_e2m1fn_x4
COPY = mybir.ActivationFunctionType.Copy
GELU = mybir.ActivationFunctionType.Gelu_apprx_tanh

P = 128
PACK = 4
LINE = 4
EDGES = 128
CHUNKS = V // EDGES
SRC, DST, EDGE = 0, 1, 2

X_LAST = 512
X_WIDTHS = ((T - X_LAST) // 2, (T - X_LAST) // 2, X_LAST)
E_WIDTHS = (2 * EDGES, EDGES, EDGES)

FREE_SHARE = 11
X_MIDDLE_ON_VECTOR = 256
W_ON_VECTOR = (0, 48, 64)


def tile_picked_edgeup_gelu_e_kernel(tc, xT, eT, w1, w2, w3, w4_words, w4_scales, offs, out):
    nc = tc.nc

    def copy(on_vector, dst, src):
        if on_vector:
            nc.vector.tensor_copy(out=dst, in_=src)
        else:
            nc.scalar.activation(out=dst, in_=src, func=COPY)

    def shared_copy(dst, src, on_vector):
        count = src.shape[1]
        cut = count - on_vector
        copy(False, dst[:, 0:cut], src[:, 0:cut])
        if on_vector > 0:
            copy(True, dst[:, cut:count], src[:, cut:count])

    def quantize(codes, scales, values):
        nc.vector.quantize_mx(out=codes.bitcast(FP8X4), scales=scales, in_=values)

    def weave(dst, first_and_second):
        nc.vector.tensor_copy(out=dst.bitcast(I32).rearrange("p (n u) -> p n u", u=2), in_=first_and_second)

    with ExitStack() as ctx:
        keep = ctx.enter_context(tc.tile_pool(name="keep", bufs=1))
        psum = ctx.enter_context(tc.psum_pool(name="psum", bufs=1))

        offsets = keep.tile([P, 2 * V // 16], U16, name="offsets")

        warm = keep.tile([P, 2], F32, name="warm")
        nc.vector.memset(warm[:, 0:1], 0.0)
        nc.scalar.activation(out=warm[:, 1:2], in_=warm[:, 0:1], func=GELU)

        planes = keep.tile([P, H], U8, name="planes", align_bytes=64)
        for q in range(P // 32):
            nc.scalar.dma_start(
                out=planes[32 * q : 32 * q + 4, 0:N].bitcast(I32),
                in_=w4_scales[0, 4 * q : 4 * q + 4, :].bitcast(I32),
            )

        x_rows = xT.rearrange("(p j) c -> p j c", j=PACK)
        x_low = keep.tile([P, 2, T], F32, name="x_low")
        nc.sync.dma_start(out=x_low[:], in_=x_rows[:, 0:2, :])
        nc.sync.dma_start(offsets[:], offs)
        x_ranges = [slice(sum(X_WIDTHS[:r]), sum(X_WIDTHS[: r + 1])) for r in range(len(X_WIDTHS))]
        x_high = []
        for r, width in enumerate(X_WIDTHS):
            x_high.append(keep.tile([P, 2, width], F32, name=f"x_high{r}"))
            nc.sync.dma_start(out=x_high[r][:], in_=x_rows[:, 2:4, x_ranges[r]])

        w_raw = [keep.tile([P, PACK, H], F32, name=f"w_raw{n}") for n in (SRC, DST, EDGE)]
        e_raw = [keep.tile([P, PACK, width], F32, name=f"e_raw{r}") for r, width in enumerate(E_WIDTHS)]
        w4_codes = keep.tile([P, 2 * N], U8, name="w4_codes", align_bytes=64)
        for n, w in enumerate((w1, w2, w3)):
            nc.sync.dma_start(out=w_raw[n][:], in_=w.rearrange("(p j) c -> p j c", j=PACK))
        e_rows = eT.rearrange("(p j) c -> p j c", j=PACK)
        for r, width in enumerate(E_WIDTHS):
            first = sum(E_WIDTHS[:r])
            nc.sync.dma_start(out=e_raw[r][:], in_=e_rows[:, :, first : first + width])
        nc.sync.dma_start(out=w4_codes[:].bitcast(I32), in_=w4_words[0].bitcast(I32))

        pairs = [keep.tile([P, 2 * T], BF16, name=f"pairs{u}", align_bytes=64) for u in range(2)]
        picked = [keep.tile([P, PACK * V], BF16, name=f"picked{n}", align_bytes=64) for n in (SRC, DST)]
        x_codes = [keep.tile([P, V], U32, name=f"x_codes{n}", align_bytes=64) for n in (SRC, DST)]
        x_scales = [keep.tile([P, V], U8, name=f"x_scales{n}", align_bytes=64) for n in (SRC, DST)]
        gathered = keep.tile([P, 2 * 2 * V], U32, name="gathered")

        def round_pairs(u, nodes, raw, on_vector):
            dst = pairs[u][:].rearrange("p (c a) -> p c a", a=2)[:, nodes, :]
            shared_copy(dst, raw[:].rearrange("p a c -> p c a"), on_vector)

        def gather(u, begin, end):
            nc.vector.tensor_copy(
                out=gathered[:, u * 2 * V + begin : u * 2 * V + end],
                in_=pairs[u][:].bitcast(U32).indirect(offsets[:, begin // 16 : end // 16]),
            )

        round_pairs(0, slice(0, T), x_low, T * FREE_SHARE // 16)
        gather(0, 0, 2 * V)
        for r, on_vector in enumerate((0, X_MIDDLE_ON_VECTOR, X_LAST * FREE_SHARE // 16)):
            round_pairs(1, x_ranges[r], x_high[r], on_vector)
        for n in (SRC, DST):
            gather(1, n * V, (n + 1) * V)
        both_pairs = gathered[:].bitcast(I32).rearrange("p (u n) -> p n u", u=2)
        for n in (SRC, DST):
            weave(picked[n][:], both_pairs[:, n * V : (n + 1) * V, :])
        for n in (SRC, DST):
            quantize(x_codes[n][:], x_scales[n][:], picked[n][:])

        w_grouped = [keep.tile([P, PACK * H], BF16, name=f"w_grouped{n}", align_bytes=64) for n in (SRC, DST, EDGE)]
        w_codes = [keep.tile([P, H], U32, name=f"w_codes{n}", align_bytes=64) for n in (SRC, DST, EDGE)]
        w_scales = [planes[4:P, :]] + [keep.tile([P, H], U8, name=f"w_scales{n}", align_bytes=64)[:] for n in (DST, EDGE)]
        e_grouped = [keep.tile([P, PACK * EDGES], BF16, name=f"e_grouped{c}", align_bytes=64) for c in range(CHUNKS)]
        e_codes = [keep.tile([P, EDGES], U32, name=f"e_codes{c}", align_bytes=64) for c in range(CHUNKS)]
        e_scales = [keep.tile([P, EDGES], U8, name=f"e_scales{c}", align_bytes=64) for c in range(CHUNKS)]
        e_chunks = [e_raw[r][:, :, first : first + EDGES] for r, width in enumerate(E_WIDTHS) for first in range(0, width, EDGES)]

        def round_weights(n):
            dst = w_grouped[n][:].rearrange("p (t m j) -> p m j t", t=PACK, j=PACK)
            src = w_raw[n][:].rearrange("p j (m t) -> p m j t", t=PACK)
            shared_copy(dst, src, W_ON_VECTOR[n])

        def quantize_weights(n, t_begin, t_end):
            cols = slice(t_begin * P, t_end * P)
            quantize(w_codes[n][:, cols], w_scales[n][:, cols], w_grouped[n][:, PACK * t_begin * P : PACK * t_end * P])

        def round_edges(c):
            dst = e_grouped[c][:].rearrange("p (g a j) -> p g j a", a=LINE, j=PACK)
            src = e_chunks[c].rearrange("p j (g a) -> p g j a", a=LINE)
            copy(c in (0, CHUNKS - 1), dst, src)

        def quantize_edges(c):
            quantize(e_codes[c][:], e_scales[c][:], e_grouped[c][:])

        banks = [f"bank{c}_{b}" for c in range(CHUNKS) for b in range(2)]
        hidden = [[psum.tile([P, 2 * EDGES], F32, name=f"hidden{c}_{b}", tag=banks[2 * c + b]) for b in range(2)] for c in range(CHUNKS)]

        def first_layer_pass(c, t, n):
            edges = slice(c * EDGES, (c + 1) * EDGES)
            cols = slice(t * P, (t + 1) * P)
            codes, scales = (e_codes[c][:], e_scales[c][:]) if n == EDGE else (x_codes[n][:, edges], x_scales[n][:, edges])
            nc.tensor.matmul_mx(
                out=hidden[c][t // 2][:, (t % 2) * EDGES : (t % 2 + 1) * EDGES],
                lhsT=w_codes[n][:, cols].bitcast(FP8X4),
                lhsT_scale=w_scales[n][:, cols],
                rhs=codes.bitcast(FP8X4),
                rhs_scale=scales,
                start=(n == SRC),
                stop=(n == EDGE),
            )

        for n in (SRC, DST):
            round_weights(n)
            quantize_weights(n, 0, PACK)
            for c in range(CHUNKS):
                for b in range(2):
                    first_layer_pass(c, 2 * b, n)

        round_weights(EDGE)
        round_edges(0)
        quantize_weights(EDGE, 0, 2)
        quantize_edges(0)
        quantize_weights(EDGE, 2, PACK)
        for c in range(1, CHUNKS):
            round_edges(c)
            quantize_edges(c)

        h_grouped = [keep.tile([P, PACK * EDGES], BF16, name=f"h_grouped{c}", align_bytes=64) for c in range(CHUNKS)]
        for c in range(CHUNKS):
            h_pairs = keep.tile([P, PACK * EDGES], BF16, name=f"h_pairs{c}")
            for b in range(2):
                first_layer_pass(c, 2 * b, EDGE)
                for n in (SRC, DST, EDGE):
                    first_layer_pass(c, 2 * b + 1, n)
                nc.scalar.activation(
                    out=h_pairs[:, b * 2 * EDGES : (b + 1) * 2 * EDGES].rearrange("p (v a) -> p v a", a=2),
                    in_=hidden[c][b][:].rearrange("p (a v) -> p v a", a=2),
                    func=GELU,
                )
            weave(h_grouped[c][:], h_pairs[:].bitcast(I32).rearrange("p (b v) -> p v b", b=2))

        out_rows = out.rearrange("(m p) v -> p m v", p=P)
        for c in range(CHUNKS):
            h_codes = keep.tile([P, EDGES], U32, name=f"h_codes{c}", align_bytes=64)
            h_scales = keep.tile([P, EDGES], U8, name=f"h_scales{c}", align_bytes=64)
            staged = keep.tile([P, 2 * EDGES], F32, name=f"staged{c}")
            quantize(h_codes[:], h_scales[:], h_grouped[c][:])
            last = c == CHUNKS - 1
            results = [psum.tile([P, 2 * EDGES], F32, name=f"result{c}_{m}", tag=banks[c + m]) for m in range(2 if last else 1)]
            for m in range(N // P):
                cols = slice(m * EDGES, (m + 1) * EDGES)
                nc.tensor.matmul_mx(
                    out=results[m if last else 0][:, cols],
                    lhsT=w4_codes[:, 2 * m * P : 2 * (m + 1) * P].bitcast(FP4X4),
                    lhsT_scale=planes[:, m * P : (m + 1) * P],
                    rhs=h_codes[:].bitcast(FP8X4),
                    rhs_scale=h_scales[:],
                    start=True,
                    stop=True,
                )
                if last:
                    copy(m == 1, staged[:, cols], results[m][:, cols])
            if not last:
                copy(False, staged[:], results[0][:])
            nc.sync.dma_start(
                out=out_rows[:, :, c * EDGES : (c + 1) * EDGES],
                in_=staged[:].rearrange("p (m v) -> p m v", m=2),
            )
